import numpy as np
CORES = [2,3,10,11,18,19,26,27,34,35,42,43,50,51,58,59]
N = 16
T = 128
ROUTE = [[[12,0,3,8],[15,4,1,3],[12,6,4,7],[2,5,15,4],[9,7,14,13],[1,2,13,0],[8,1,2,13],[15,8,11,1],[12,7,3,14],[13,14,10,0],[0,9,11,1],[2,13,10,12],[10,2,4,7],[1,8,6,4],[14,15,10,11],[7,12,14,9],[1,10,0,7],[0,7,3,1],[8,6,4,12],[4,2,8,15],[0,14,1,4],[9,14,12,10],[11,0,1,12],[4,8,11,10],[1,7,5,2],[11,2,7,4],[9,2,11,10],[11,12,6,2],[8,6,10,3],[0,13,11,7],[2,14,9,13],[5,8,2,9],[15,6,5,0],[4,14,12,10],[12,10,13,14],[13,6,5,9],[7,4,0,15],[10,6,5,12],[10,9,6,2],[2,4,8,5],[5,15,10,8],[10,4,5,7],[5,4,7,13],[8,10,6,11],[8,14,0,9],[5,11,2,14],[13,1,10,4],[5,1,4,3],[13,14,1,3],[8,9,3,14],[15,4,7,0],[13,0,11,12],[10,12,9,14],[15,9,10,0],[15,7,13,3],[9,1,0,14],[0,6,14,4],[6,3,15,9],[4,5,14,1],[6,8,4,1],[1,4,14,6],[15,13,8,7],[14,5,9,7],[6,2,11,15],[8,13,12,6],[6,1,5,0],[12,15,0,5],[2,1,5,3],[9,13,12,1],[0,12,10,14],[2,4,3,15],[3,4,13,5],[14,0,11,8],[9,5,0,7],[5,3,13,2],[5,6,1,3],[9,0,8,5],[0,6,12,4],[9,8,6,7],[6,12,11,3],[10,14,1,8],[11,13,10,6],[6,9,2,8],[9,1,10,7],[0,10,14,3],[13,10,14,12],[12,7,4,6],[13,14,2,6],[10,6,1,9],[15,12,5,10],[11,14,3,13],[12,3,15,7],[0,6,9,4],[5,1,10,6],[4,10,0,14],[5,12,6,9],[8,7,1,10],[0,4,6,5],[11,13,8,15],[3,15,4,8],[8,5,10,11],[3,13,1,15],[5,0,8,6],[0,7,11,14],[3,11,7,14],[6,8,1,0],[6,4,12,8],[8,9,7,15],[7,10,8,4],[6,0,13,12],[0,5,9,14],[14,7,2,11],[3,11,14,4],[0,3,2,11],[13,8,14,5],[8,1,12,4],[7,15,12,3],[8,10,4,14],[6,9,5,13],[12,0,4,1],[13,6,7,0],[0,2,11,4],[11,14,8,3],[5,2,9,7],[11,15,14,5],[7,10,3,1],[5,3,6,0],[13,1,7,15]],[[7,10,14,8],[11,10,13,14],[2,6,12,9],[6,10,9,11],[14,11,9,12],[2,4,12,11],[9,1,13,15],[4,7,11,1],[11,9,3,10],[5,3,2,1],[3,1,9,15],[15,9,1,13],[0,8,12,7],[3,9,2,8],[3,0,1,10],[0,12,2,14],[9,3,5,0],[1,9,12,8],[8,5,3,14],[15,7,1,3],[10,13,9,11],[0,3,5,7],[2,6,1,10],[9,1,7,10],[5,10,4,13],[13,8,10,6],[13,14,5,2],[0,11,12,8],[7,1,12,15],[12,10,3,7],[14,6,9,12],[8,5,13,14],[13,8,14,1],[9,8,1,10],[10,4,3,0],[0,5,8,9],[2,7,8,12],[9,13,12,2],[13,2,14,4],[3,9,4,7],[6,12,2,4],[14,12,8,11],[15,0,11,2],[11,4,1,10],[12,5,8,3],[3,15,7,1],[4,11,3,10],[0,11,12,14],[8,13,14,10],[14,11,15,10],[14,4,1,5],[1,14,13,5],[1,4,8,11],[4,14,8,10],[3,9,11,0],[5,10,8,2],[9,15,5,11],[12,9,5,6],[6,11,9,1],[4,9,2,14],[8,9,7,13],[5,15,0,4],[13,3,1,9],[12,8,9,0],[3,1,5,9],[14,12,2,5],[9,1,15,8],[9,2,11,8],[6,7,8,15],[12,14,5,8],[7,10,3,0],[1,13,8,5],[2,9,10,4],[10,3,5,0],[14,6,2,7],[12,9,8,5],[10,7,4,14],[6,8,12,7],[13,4,3,0],[2,9,11,3],[13,9,3,2],[6,4,0,7],[0,5,11,7],[14,6,13,5],[0,8,7,1],[8,6,9,7],[13,0,11,14],[2,11,1,9],[6,10,9,12],[0,11,15,1],[8,3,5,9],[15,12,9,7],[9,12,4,6],[0,13,2,3],[8,4,3,13],[11,8,7,5],[7,6,3,8],[7,12,4,13],[9,4,2,1],[12,9,7,4],[6,2,13,5],[15,5,2,0],[13,11,4,0],[0,13,11,1],[7,2,0,9],[13,6,3,5],[9,8,3,4],[2,15,12,8],[3,14,7,0],[12,9,7,15],[13,1,10,0],[0,4,5,10],[7,8,12,5],[12,1,6,3],[7,8,2,0],[8,6,5,0],[4,6,7,13],[13,3,8,10],[12,15,5,14],[14,6,0,2],[2,15,6,0],[12,2,9,10],[8,12,3,14],[4,2,8,10],[0,6,8,13],[12,6,3,4],[13,5,7,15],[6,4,1,11]],[[4,2,6,5],[10,9,1,5],[15,3,9,8],[6,9,14,10],[13,9,3,2],[3,14,8,4],[1,14,13,8],[0,9,15,10],[1,3,9,11],[10,5,15,8],[5,14,11,13],[4,15,11,13],[6,11,7,4],[15,1,0,10],[1,2,6,15],[12,7,5,0],[14,0,3,5],[4,12,8,0],[7,10,14,11],[6,8,4,1],[0,14,12,10],[14,5,6,15],[1,10,9,2],[5,1,14,3],[15,9,11,13],[13,10,6,15],[4,9,6,2],[12,5,8,13],[12,6,13,11],[9,13,5,12],[2,11,13,0],[1,15,3,13],[1,5,4,15],[13,5,10,2],[8,14,15,2],[3,6,13,4],[7,5,1,8],[13,12,1,9],[2,0,9,14],[5,11,2,1],[8,10,5,14],[2,15,7,14],[8,11,15,10],[10,15,5,3],[14,3,6,0],[11,7,13,9],[0,3,14,1],[1,14,5,0],[10,3,5,12],[1,7,6,11],[12,1,11,10],[1,5,6,7],[12,1,4,2],[9,8,14,1],[15,13,9,11],[1,11,0,6],[1,9,5,2],[5,3,1,14],[8,11,1,13],[3,15,8,13],[14,0,6,2],[8,5,3,4],[15,5,1,2],[2,6,5,8],[9,3,8,4],[13,10,9,11],[5,9,13,11],[13,10,6,7],[1,9,11,4],[12,15,11,8],[9,10,1,14],[4,2,1,14],[4,13,6,3],[0,3,10,1],[8,0,15,2],[4,9,1,13],[12,1,14,5],[6,14,0,3],[7,9,13,12],[10,14,0,2],[3,14,10,1],[8,0,14,4],[0,3,2,1],[9,12,3,6],[3,6,11,15],[14,15,2,8],[10,0,7,15],[9,3,11,13],[11,4,1,8],[3,12,15,8],[5,10,4,3],[8,3,12,9],[6,7,14,1],[8,2,4,0],[11,10,3,13],[5,11,6,2],[9,13,10,3],[0,5,7,3],[11,9,14,15],[2,4,0,6],[3,4,13,0],[0,7,15,12],[4,11,5,0],[4,12,1,2],[8,1,12,11],[2,11,4,14],[9,8,11,5],[10,13,6,7],[14,15,9,0],[15,10,11,14],[12,3,4,14],[1,5,3,7],[4,9,2,15],[8,1,4,10],[15,10,13,14],[14,0,4,12],[11,1,10,7],[3,12,13,2],[6,1,2,13],[6,10,2,0],[4,15,12,6],[6,4,8,1],[14,12,7,6],[9,14,13,4],[1,8,13,7],[12,0,7,9],[4,3,6,13],[14,5,10,6]],[[0,14,15,5],[2,5,3,11],[7,12,9,10],[10,9,7,3],[9,12,8,1],[7,0,2,5],[15,6,13,8],[11,1,2,15],[3,1,2,13],[13,7,12,6],[2,3,8,10],[3,5,10,2],[6,13,14,4],[4,2,1,14],[9,3,0,14],[13,0,12,9],[11,15,5,9],[5,9,13,3],[9,6,15,0],[7,9,6,10],[3,8,2,11],[15,2,0,14],[0,1,11,10],[13,0,9,5],[15,9,10,13],[1,7,10,5],[8,0,6,13],[0,14,5,11],[10,8,5,2],[4,3,8,10],[10,6,13,2],[13,1,8,9],[4,13,6,7],[3,14,5,4],[13,4,3,1],[7,5,11,8],[15,14,6,1],[2,14,4,11],[10,1,5,11],[7,11,9,4],[8,9,5,2],[14,6,15,5],[4,1,2,8],[9,7,0,3],[8,0,15,6],[7,9,12,6],[5,13,7,1],[8,13,14,15],[0,5,7,12],[6,8,2,10],[4,7,10,8],[2,5,8,10],[1,13,7,8],[1,14,4,7],[15,3,9,11],[12,15,3,1],[15,7,3,14],[11,1,6,14],[12,8,3,9],[6,7,2,13],[0,10,13,8],[11,9,5,1],[15,0,9,8],[7,15,9,14],[6,15,7,11],[14,9,15,10],[3,1,12,14],[1,3,14,13],[12,4,14,7],[3,1,14,0],[15,8,14,6],[1,10,14,7],[13,0,5,14],[5,3,6,11],[2,7,8,9],[5,0,3,13],[11,12,14,2],[13,3,8,9],[4,11,8,1],[4,12,6,13],[15,14,11,2],[10,11,2,3],[1,0,4,10],[7,6,5,9],[12,0,2,9],[14,9,0,6],[15,13,10,7],[6,1,13,14],[12,13,1,4],[7,10,11,4],[15,12,8,9],[10,12,9,14],[15,3,10,4],[1,9,0,10],[1,3,5,8],[9,6,10,7],[0,4,7,12],[6,14,8,13],[8,7,4,0],[3,4,15,14],[2,14,11,13],[1,9,12,8],[10,0,1,9],[13,14,12,6],[5,0,11,7],[12,11,0,6],[9,5,15,14],[7,12,15,13],[5,1,10,2],[0,3,1,14],[2,5,10,8],[13,4,15,5],[4,5,1,7],[6,9,3,13],[0,3,14,6],[5,8,6,14],[5,10,2,0],[6,1,4,11],[10,4,3,15],[6,14,10,1],[7,14,15,3],[3,5,7,15],[10,14,12,2],[11,8,5,6],[4,13,8,1],[12,15,10,13],[1,10,2,11],[0,15,7,11]],[[1,4,12,13],[3,13,0,10],[4,10,3,8],[10,9,14,15],[12,3,1,6],[3,4,8,2],[4,3,13,15],[3,15,7,13],[15,5,9,7],[13,1,8,4],[0,8,9,5],[8,1,13,4],[10,4,5,13],[3,14,9,2],[11,7,8,5],[1,5,3,15],[1,7,15,9],[7,15,12,6],[3,9,13,0],[6,9,5,3],[6,10,0,2],[3,4,2,13],[1,14,15,9],[0,2,5,14],[8,5,7,0],[4,12,15,1],[1,2,8,13],[0,1,4,3],[8,2,6,13],[0,15,3,11],[10,13,1,3],[15,5,4,0],[0,4,15,11],[12,6,5,14],[11,1,0,14],[4,15,2,10],[15,11,2,3],[13,14,8,11],[5,13,2,11],[10,3,11,7],[4,11,1,0],[1,8,4,7],[2,4,6,7],[14,9,1,13],[2,10,12,14],[2,15,14,10],[7,0,13,15],[4,8,0,14],[7,0,12,6],[15,11,0,1],[0,3,11,5],[13,1,2,12],[3,8,15,10],[15,4,11,6],[6,7,10,13],[6,14,3,8],[7,10,5,0],[3,9,2,4],[11,4,15,12],[0,15,9,10],[0,6,15,1],[2,15,10,3],[14,10,2,8],[9,10,2,8],[0,2,1,9],[12,11,14,5],[11,5,7,9],[1,3,6,14],[13,9,1,8],[2,4,8,13],[14,8,4,13],[10,8,14,2],[2,12,5,9],[1,11,15,2],[5,14,13,1],[15,12,14,9],[2,15,12,14],[14,8,15,9],[15,1,11,6],[3,4,2,12],[3,6,4,7],[15,13,6,1],[12,3,10,5],[13,10,3,4],[12,6,2,9],[10,13,15,14],[15,4,9,8],[4,7,14,13],[8,15,9,10],[10,11,3,2],[1,12,9,5],[4,0,15,2],[6,11,3,8],[5,3,7,0],[12,3,13,10],[11,0,12,4],[8,4,5,15],[0,1,11,15],[12,1,2,6],[2,13,7,8],[3,2,4,12],[2,6,8,4],[15,9,14,3],[11,4,15,8],[14,13,7,9],[14,4,10,1],[13,0,9,4],[10,4,12,6],[14,7,4,6],[2,1,8,4],[1,11,9,15],[14,4,7,15],[10,4,7,5],[7,9,5,14],[12,7,4,6],[5,11,1,15],[4,15,0,14],[9,5,1,10],[15,10,12,14],[13,6,3,12],[9,11,14,1],[10,11,14,13],[7,12,0,10],[14,7,1,9],[11,2,3,8],[4,0,3,9],[5,14,7,15],[9,15,14,4]],[[0,5,9,10],[5,0,7,2],[1,8,6,11],[1,13,15,6],[11,3,6,4],[3,6,2,0],[4,9,11,13],[9,3,14,11],[4,11,8,9],[0,5,8,4],[15,13,3,12],[6,5,4,13],[5,9,1,15],[9,14,0,6],[2,0,1,4],[12,7,10,15],[13,2,6,0],[2,3,5,7],[0,2,3,8],[6,4,13,5],[6,8,5,14],[15,14,13,1],[15,1,11,9],[10,11,14,0],[0,6,14,5],[10,9,7,2],[5,11,2,3],[10,5,6,11],[2,11,9,0],[5,4,11,2],[4,0,3,6],[8,5,12,10],[8,13,7,12],[11,10,2,14],[4,9,6,7],[0,12,14,5],[4,10,1,13],[12,2,4,9],[6,13,15,12],[13,12,3,14],[9,6,7,5],[4,13,12,0],[10,3,11,14],[4,5,0,6],[9,1,2,10],[2,5,6,14],[5,12,3,6],[14,0,1,15],[8,11,14,4],[4,8,7,1],[3,11,8,10],[6,11,15,14],[11,6,4,14],[9,4,12,2],[13,9,14,11],[12,7,8,4],[11,4,5,6],[5,3,11,13],[4,9,3,2],[1,11,15,4],[14,3,13,11],[5,14,4,6],[9,4,13,6],[8,0,12,10],[8,3,0,4],[9,14,2,1],[5,14,9,15],[9,0,3,14],[4,10,7,6],[2,6,5,11],[10,4,7,13],[6,0,2,11],[3,11,4,7],[8,13,15,7],[7,14,13,12],[6,12,3,15],[0,2,14,6],[7,2,12,13],[8,7,5,3],[0,2,7,5],[7,9,10,15],[5,8,15,13],[15,10,8,14],[5,11,3,7],[10,3,7,13],[3,5,12,7],[9,2,5,7],[4,5,2,11],[6,15,3,13],[3,11,0,14],[6,11,13,5],[13,9,0,2],[1,7,0,2],[4,1,8,5],[13,10,12,3],[7,14,5,15],[4,15,8,5],[1,7,11,6],[10,15,8,3],[5,4,13,2],[5,6,9,2],[6,8,7,4],[13,14,15,12],[7,12,1,14],[3,8,15,1],[15,2,14,9],[15,12,6,9],[0,11,3,6],[1,11,15,13],[0,8,4,15],[9,10,12,3],[10,5,8,2],[11,1,15,0],[5,0,3,13],[9,12,10,13],[5,10,2,13],[13,0,2,3],[11,3,13,7],[6,3,8,10],[0,15,4,10],[13,6,14,2],[4,13,14,11],[11,10,0,12],[4,7,6,15],[10,9,5,14],[0,1,11,7],[10,4,12,15],[7,10,11,1]],[[14,15,0,4],[1,14,15,12],[1,13,15,3],[6,13,11,15],[7,10,14,3],[9,15,8,2],[1,12,3,10],[6,12,0,3],[6,11,3,13],[3,9,0,11],[0,15,2,13],[9,3,8,14],[0,10,14,2],[12,15,11,13],[3,5,6,2],[2,4,0,5],[9,12,3,11],[2,5,8,4],[4,14,6,15],[6,8,7,0],[8,15,2,11],[15,13,3,12],[3,0,5,12],[2,11,4,9],[6,13,3,2],[0,13,10,6],[0,13,15,1],[11,4,5,0],[2,10,11,15],[14,6,3,10],[0,6,11,14],[0,15,11,8],[11,12,5,3],[1,8,4,0],[13,0,3,7],[6,10,7,8],[14,6,7,1],[1,4,0,14],[6,14,12,3],[3,9,5,6],[2,9,5,13],[2,8,1,0],[2,15,11,6],[12,8,0,7],[5,10,13,0],[3,1,6,9],[3,8,9,11],[4,13,2,6],[2,6,10,9],[13,5,9,10],[13,10,6,9],[5,3,10,6],[11,15,9,13],[6,15,11,9],[5,3,13,9],[5,14,6,15],[14,4,3,1],[14,0,8,7],[5,12,7,3],[10,9,7,11],[0,15,12,4],[6,9,3,12],[14,11,12,9],[1,9,4,12],[7,6,4,5],[10,2,0,4],[2,11,13,6],[7,12,5,4],[12,1,4,15],[10,8,7,11],[4,13,2,12],[9,11,7,14],[6,11,5,10],[14,6,4,2],[11,15,6,9],[10,2,12,3],[4,14,2,1],[13,15,3,7],[5,0,9,6],[1,12,3,7],[6,9,4,14],[10,4,1,3],[3,9,14,7],[13,10,6,7],[13,9,5,7],[8,13,14,9],[2,8,13,7],[12,1,6,5],[11,1,6,14],[15,3,0,10],[12,1,5,7],[13,4,8,2],[2,15,14,13],[3,1,0,13],[11,1,6,0],[11,15,4,1],[9,5,11,7],[15,0,8,9],[8,9,3,1],[10,1,11,3],[3,13,10,4],[3,0,10,4],[12,9,8,2],[0,4,11,7],[2,0,6,11],[11,13,1,2],[0,6,13,15],[0,5,2,13],[11,1,10,14],[4,0,13,14],[9,6,2,14],[9,15,14,11],[12,5,13,3],[0,3,12,10],[15,3,2,14],[9,13,11,3],[10,2,11,15],[14,7,5,15],[1,13,0,14],[10,9,3,5],[10,8,5,6],[5,15,7,10],[10,13,11,15],[3,8,5,6],[2,14,13,4],[12,4,9,7],[14,13,7,8],[8,12,15,5]],[[2,11,14,8],[9,6,10,0],[11,1,15,13],[15,5,1,0],[6,14,3,2],[6,11,8,1],[11,1,3,6],[4,2,11,5],[6,5,15,11],[12,15,5,7],[2,4,10,15],[6,11,1,3],[14,7,3,4],[15,8,9,7],[4,15,12,2],[12,15,11,8],[13,12,8,9],[9,15,4,13],[4,2,5,11],[14,7,0,11],[8,13,11,15],[11,8,12,9],[15,13,10,14],[9,8,14,1],[14,1,11,8],[15,6,7,14],[4,11,8,3],[5,7,11,8],[14,4,2,11],[13,4,14,11],[5,6,4,9],[5,3,13,8],[5,11,13,2],[1,0,6,7],[13,7,8,10],[0,9,12,13],[7,14,1,11],[7,15,2,14],[5,11,4,2],[10,5,2,7],[1,4,6,15],[7,1,8,15],[5,2,9,3],[14,12,13,11],[6,13,9,14],[1,14,13,3],[1,3,10,13],[13,10,9,14],[8,5,3,10],[14,0,9,13],[3,7,4,2],[13,10,8,4],[5,7,3,4],[5,4,11,7],[7,11,8,15],[0,14,12,5],[9,2,8,6],[4,8,2,11],[4,12,5,6],[12,3,8,7],[11,9,5,15],[11,12,5,2],[15,13,5,14],[0,1,4,14],[12,7,3,13],[15,3,12,9],[13,4,15,6],[14,8,9,2],[2,12,8,4],[8,10,1,7],[4,13,14,7],[15,2,12,11],[4,8,7,1],[7,13,0,15],[13,5,7,15],[2,1,15,13],[5,14,1,9],[3,11,9,10],[2,8,4,9],[1,10,8,9],[8,2,3,9],[1,5,3,9],[13,12,0,11],[11,13,10,12],[7,13,3,15],[2,5,1,6],[9,7,14,8],[10,13,4,1],[10,6,3,12],[7,2,14,13],[14,13,7,10],[13,15,11,2],[15,6,1,9],[8,10,4,12],[11,6,8,1],[6,8,15,13],[14,4,13,15],[9,3,8,2],[10,12,11,1],[11,15,10,8],[11,15,14,2],[13,9,12,2],[11,14,9,2],[4,11,5,12],[1,2,14,15],[3,7,6,15],[4,11,5,10],[3,14,11,8],[13,2,5,10],[7,14,9,8],[4,14,3,1],[6,9,2,10],[9,10,11,0],[1,7,5,13],[4,15,11,8],[15,0,10,14],[1,9,14,5],[12,8,5,15],[15,6,8,5],[13,2,7,8],[14,13,6,3],[9,5,1,7],[8,4,15,12],[2,11,0,8],[4,10,13,11],[11,5,14,13],[7,6,9,14],[11,5,15,10]],[[15,0,8,3],[1,15,4,8],[11,0,5,14],[13,11,5,3],[3,14,2,15],[1,2,14,10],[14,3,6,11],[10,11,15,6],[7,6,1,0],[8,6,0,12],[7,8,1,9],[13,15,5,10],[3,4,6,14],[8,7,1,5],[10,4,2,14],[5,14,4,10],[7,12,13,6],[6,13,11,14],[11,15,4,13],[3,12,14,7],[7,15,13,1],[7,13,2,8],[8,9,6,0],[2,6,1,4],[9,10,14,11],[10,11,6,9],[1,9,8,15],[7,2,3,8],[15,5,13,14],[7,2,12,4],[2,15,11,13],[8,2,4,5],[14,6,3,8],[5,3,2,4],[15,10,7,5],[1,3,4,15],[5,11,3,12],[11,15,2,14],[12,0,9,1],[3,6,14,12],[12,0,13,11],[9,10,3,1],[13,15,12,2],[13,3,15,6],[5,3,8,10],[2,5,10,13],[0,7,3,5],[11,3,7,13],[15,11,5,8],[6,1,12,3],[7,13,8,11],[8,5,6,4],[8,3,2,6],[8,9,7,6],[6,15,14,4],[4,12,2,7],[8,1,5,9],[12,11,8,3],[12,3,10,5],[15,7,10,0],[6,11,4,5],[5,6,7,8],[0,12,11,14],[2,9,4,13],[4,2,0,10],[4,12,11,9],[3,2,4,1],[15,3,7,2],[10,11,1,8],[9,7,4,11],[2,7,15,1],[6,10,0,13],[6,0,13,15],[5,9,14,3],[13,5,4,1],[0,8,3,9],[3,1,14,8],[3,11,0,6],[8,13,0,9],[9,14,6,8],[12,2,0,10],[11,0,4,14],[11,13,2,12],[9,1,15,14],[9,2,14,5],[6,3,4,5],[8,7,5,6],[3,6,14,1],[13,2,11,8],[13,4,2,0],[4,8,15,0],[7,11,5,3],[9,13,4,3],[1,7,5,9],[3,13,10,8],[10,7,14,2],[13,3,4,5],[0,4,13,7],[14,1,7,13],[10,9,14,13],[12,0,1,3],[0,5,3,14],[15,11,12,13],[12,2,15,4],[11,15,12,14],[10,5,6,15],[6,12,3,4],[14,9,5,13],[5,7,8,0],[6,8,1,2],[7,10,5,6],[14,1,12,15],[3,5,1,7],[12,2,5,3],[14,0,9,6],[5,0,2,3],[15,12,4,9],[1,15,11,8],[6,10,1,11],[6,10,0,11],[4,9,15,7],[4,2,13,15],[14,15,12,9],[8,9,7,0],[8,1,9,14],[13,3,9,2],[7,5,15,3],[4,6,9,12]],[[13,5,1,9],[0,1,14,4],[14,0,13,2],[11,3,8,7],[3,8,1,0],[3,0,5,4],[13,11,9,5],[5,13,8,12],[6,3,8,0],[8,7,14,1],[9,1,2,8],[4,15,5,8],[7,11,15,12],[3,1,4,9],[7,6,2,5],[14,6,1,8],[15,0,7,3],[4,0,2,6],[1,5,10,6],[6,14,5,2],[12,0,3,9],[8,12,15,10],[8,0,2,13],[14,11,0,3],[0,12,1,7],[9,13,1,6],[7,13,14,0],[15,0,2,8],[9,3,4,7],[10,12,14,11],[14,7,11,10],[15,1,5,9],[4,14,10,11],[1,12,6,3],[12,9,10,0],[8,2,5,13],[0,6,13,1],[10,13,7,8],[6,13,12,15],[11,0,15,6],[13,12,0,9],[3,15,5,1],[9,10,8,0],[0,4,1,2],[15,12,0,6],[15,13,3,8],[7,3,10,6],[15,10,14,2],[6,12,5,4],[11,7,15,8],[3,5,6,15],[13,9,8,0],[12,11,6,8],[11,15,14,9],[4,3,1,2],[15,10,1,5],[2,0,11,4],[11,2,14,9],[2,3,6,11],[5,4,7,1],[6,1,2,12],[10,13,3,5],[15,14,7,4],[13,6,3,15],[3,14,4,10],[3,11,8,10],[14,13,15,12],[14,2,4,10],[0,11,4,2],[15,4,12,5],[6,14,5,0],[7,10,12,5],[11,0,15,14],[1,7,6,2],[6,5,11,0],[9,13,8,5],[15,4,3,5],[1,3,2,9],[8,5,9,12],[8,7,10,3],[7,13,15,9],[7,11,13,8],[4,8,12,11],[6,7,8,5],[2,1,0,15],[5,8,3,6],[8,13,11,5],[0,4,8,9],[11,3,14,12],[11,13,14,7],[13,0,8,1],[1,12,7,3],[14,3,2,13],[1,11,5,12],[3,8,7,4],[2,1,6,10],[4,12,8,10],[2,4,0,13],[6,12,3,1],[11,14,6,0],[15,5,10,12],[7,8,13,9],[7,13,6,1],[8,4,9,15],[11,0,14,2],[9,15,0,4],[6,4,15,10],[14,13,6,4],[3,10,5,8],[8,2,5,0],[7,12,1,5],[1,14,13,3],[10,2,0,4],[11,12,9,5],[0,5,12,11],[0,9,5,11],[9,1,7,11],[6,14,10,0],[7,15,4,12],[11,7,0,8],[15,1,12,13],[7,0,13,12],[0,11,10,5],[2,5,1,14],[4,7,6,1],[10,15,8,2],[8,2,14,6],[9,8,10,15]],[[3,1,8,6],[12,1,4,0],[12,15,3,13],[1,5,7,4],[5,14,6,9],[8,9,13,7],[15,10,6,1],[4,3,8,2],[8,0,2,7],[7,6,5,14],[13,7,15,12],[3,8,5,12],[2,15,5,6],[3,14,9,5],[6,11,2,0],[10,3,9,11],[10,4,12,1],[2,6,3,13],[3,1,8,13],[11,1,8,6],[14,4,3,9],[6,0,3,4],[1,11,2,15],[9,4,6,8],[9,11,3,0],[6,2,12,10],[13,3,14,8],[1,12,15,6],[6,3,13,14],[11,0,4,2],[4,6,15,0],[13,2,11,12],[10,5,9,6],[13,9,15,3],[4,5,7,8],[0,14,6,15],[15,7,4,1],[13,5,6,14],[3,10,2,9],[0,2,14,5],[10,1,12,6],[14,2,9,10],[8,4,11,10],[6,12,8,7],[7,9,12,4],[10,5,0,7],[10,7,13,9],[6,0,10,8],[8,15,0,14],[6,14,15,10],[2,0,14,8],[7,15,13,8],[2,11,5,0],[13,10,11,6],[4,14,11,7],[2,1,3,6],[9,5,4,0],[11,1,4,14],[0,13,8,9],[13,14,5,0],[0,14,6,15],[5,10,3,1],[0,3,10,15],[7,13,14,0],[6,7,14,3],[14,5,11,7],[8,1,13,15],[12,2,13,14],[4,0,13,9],[8,11,9,6],[14,10,15,7],[12,6,14,5],[1,3,14,13],[6,15,8,12],[12,4,14,9],[4,3,6,7],[0,9,4,2],[4,5,15,9],[9,14,2,3],[9,3,14,7],[2,9,10,6],[6,7,14,2],[1,4,7,12],[15,13,12,1],[14,7,0,13],[13,11,12,9],[14,2,3,15],[7,8,9,3],[9,7,10,0],[6,13,10,5],[10,7,9,0],[14,11,13,5],[2,8,10,1],[8,13,14,1],[9,8,1,6],[0,9,13,15],[2,11,1,3],[3,7,11,8],[10,13,5,1],[5,14,13,0],[14,7,2,11],[2,4,7,9],[15,14,8,5],[15,13,1,8],[5,4,10,13],[3,4,1,7],[14,11,5,13],[11,14,13,10],[13,5,0,15],[4,15,5,11],[8,5,0,13],[9,11,15,2],[9,12,2,5],[6,11,3,13],[2,13,12,1],[1,2,9,6],[11,1,3,8],[0,9,2,13],[14,15,0,12],[7,13,12,6],[7,10,13,2],[4,8,14,6],[15,0,11,1],[12,3,6,2],[13,9,8,6],[7,1,12,8],[8,14,9,13],[15,7,10,0]],[[4,13,12,14],[9,7,0,11],[13,7,6,4],[10,4,7,14],[10,5,9,15],[6,5,9,3],[7,14,2,10],[2,14,15,4],[14,7,0,3],[15,6,3,7],[13,3,7,10],[5,13,12,4],[13,1,15,8],[14,3,7,11],[3,2,11,14],[2,3,1,10],[12,4,7,2],[7,4,10,5],[13,2,8,0],[13,14,12,0],[13,9,14,4],[5,9,8,6],[0,6,3,14],[9,2,0,4],[15,0,2,11],[15,7,9,6],[5,10,7,0],[6,12,2,1],[5,2,10,3],[13,4,15,8],[12,3,14,7],[3,14,11,1],[6,15,8,0],[13,11,6,2],[1,5,2,10],[11,7,8,9],[5,11,4,13],[14,6,13,5],[14,7,2,9],[14,7,4,5],[2,5,10,7],[13,6,11,4],[11,13,4,2],[11,15,4,3],[0,2,14,10],[12,9,6,0],[5,14,13,2],[5,10,0,6],[4,10,0,11],[15,2,12,5],[13,11,5,10],[5,12,13,3],[15,4,5,8],[10,12,13,5],[9,11,4,0],[6,2,3,13],[10,3,7,13],[4,1,13,8],[3,13,15,10],[5,6,3,4],[4,10,13,2],[6,2,11,4],[6,14,11,12],[14,10,8,1],[5,8,6,7],[14,8,5,15],[1,15,0,8],[12,11,14,6],[3,14,4,5],[2,8,4,9],[6,3,7,5],[7,12,14,11],[5,11,3,2],[10,4,8,5],[1,15,12,7],[8,13,9,14],[4,14,11,3],[4,11,0,2],[5,15,2,4],[13,14,0,1],[15,11,13,3],[13,11,3,6],[11,7,3,1],[7,1,15,3],[8,15,7,13],[14,4,13,10],[5,13,3,2],[0,9,4,7],[10,7,4,12],[6,9,3,13],[10,12,13,8],[5,14,2,4],[4,1,7,2],[11,0,7,3],[0,14,2,10],[1,4,5,10],[11,0,2,8],[2,3,0,11],[15,9,10,6],[8,1,3,15],[7,3,2,5],[15,1,3,13],[14,5,10,13],[3,8,4,13],[9,12,11,1],[8,12,3,14],[14,15,9,11],[12,9,1,6],[6,7,10,11],[8,4,5,15],[1,4,9,6],[10,15,1,11],[6,5,4,1],[2,12,14,3],[6,11,14,13],[0,10,7,15],[3,6,14,2],[10,13,0,2],[14,0,2,3],[10,11,3,8],[10,1,14,7],[10,0,8,5],[1,7,11,3],[5,0,1,13],[10,8,15,12],[1,9,11,8],[14,7,4,11],[7,15,8,2]],[[1,5,12,6],[6,13,4,2],[10,3,13,9],[7,9,11,10],[10,9,2,3],[5,11,12,15],[6,8,3,2],[7,2,10,3],[0,5,8,1],[15,11,5,14],[3,4,14,1],[8,3,4,14],[1,8,7,6],[14,5,10,3],[3,5,8,11],[9,6,3,1],[15,11,7,6],[2,8,6,12],[4,9,2,15],[12,6,10,3],[1,0,11,14],[7,3,15,12],[3,13,11,6],[0,12,5,4],[12,8,11,14],[6,12,8,4],[15,12,14,5],[9,12,0,1],[6,14,0,10],[1,4,15,13],[14,9,7,11],[11,14,9,0],[11,4,13,0],[0,9,4,11],[2,1,10,9],[4,3,11,6],[5,2,15,9],[6,15,1,12],[7,2,5,12],[1,9,12,14],[4,13,10,1],[13,9,14,10],[8,0,1,10],[15,11,10,5],[13,6,2,5],[6,1,12,11],[6,15,9,13],[5,7,2,4],[15,10,9,7],[11,5,15,0],[5,14,15,10],[1,14,10,11],[7,1,12,10],[3,6,15,11],[4,14,8,13],[2,8,5,3],[15,1,13,4],[5,8,1,9],[9,7,15,0],[4,0,15,12],[8,14,9,12],[4,0,6,1],[4,7,14,2],[14,6,11,3],[3,13,9,6],[11,13,4,8],[2,1,3,11],[8,3,12,7],[5,12,3,2],[8,0,14,15],[11,4,13,12],[12,5,10,11],[0,6,8,9],[7,12,13,3],[9,15,7,6],[13,11,14,9],[0,3,2,11],[14,5,9,0],[6,5,9,13],[9,2,13,6],[2,6,0,9],[4,3,15,9],[15,14,9,1],[6,2,0,10],[8,7,15,10],[6,4,9,13],[9,4,0,1],[4,15,2,6],[6,12,9,13],[15,12,8,9],[4,5,9,0],[3,5,8,11],[7,11,3,5],[11,9,7,6],[12,7,14,9],[4,7,14,6],[4,8,13,0],[9,7,13,3],[5,4,14,9],[6,5,7,10],[7,10,5,14],[12,3,5,9],[15,9,0,1],[8,12,9,7],[14,4,13,0],[0,8,12,14],[13,11,2,10],[14,9,10,6],[6,2,0,12],[12,3,9,11],[13,9,7,10],[2,11,15,10],[12,6,2,9],[6,13,4,8],[3,5,11,4],[1,7,13,9],[8,15,13,11],[3,10,14,8],[4,11,8,14],[9,10,3,6],[7,15,1,6],[14,6,12,4],[14,4,13,10],[11,4,1,8],[0,3,12,5],[8,12,1,4],[5,4,3,15],[7,9,6,0]],[[9,0,15,13],[10,9,4,0],[4,15,2,3],[10,8,0,1],[0,3,7,2],[15,1,3,12],[10,1,3,2],[9,15,3,0],[1,8,9,13],[7,15,2,1],[14,12,11,7],[14,8,1,2],[12,10,15,6],[15,6,14,0],[5,2,6,15],[15,5,10,14],[6,3,15,11],[15,9,4,1],[5,8,7,13],[7,0,2,3],[15,7,11,4],[7,9,14,12],[5,3,13,14],[10,7,8,9],[3,8,13,5],[10,6,13,11],[1,9,5,8],[4,11,12,5],[1,13,0,11],[15,8,13,5],[7,6,9,15],[4,8,6,15],[13,4,11,0],[7,8,9,4],[4,10,11,8],[14,15,1,10],[12,4,8,2],[6,4,2,10],[12,10,2,3],[9,7,6,13],[4,15,14,0],[8,9,6,14],[0,3,11,14],[7,12,6,3],[4,3,0,11],[7,13,6,10],[15,12,10,14],[6,11,7,0],[3,12,15,6],[9,2,10,3],[6,5,1,10],[1,13,2,3],[13,1,5,2],[14,9,10,2],[11,1,7,4],[12,11,15,14],[9,2,3,12],[8,6,2,9],[10,14,3,15],[0,1,11,6],[11,9,7,0],[9,1,14,6],[4,5,10,13],[0,4,14,3],[2,0,11,3],[15,6,4,7],[6,1,15,0],[14,0,6,3],[5,3,15,7],[8,5,15,3],[14,7,12,2],[9,1,7,13],[13,5,10,7],[6,4,10,2],[6,8,0,14],[15,4,13,1],[6,3,12,11],[13,11,2,8],[4,15,14,2],[5,12,14,9],[8,1,6,15],[14,3,5,15],[7,9,5,8],[13,8,12,15],[4,10,1,14],[2,12,0,7],[8,1,2,5],[12,9,5,15],[11,7,5,10],[9,13,4,5],[3,14,9,12],[1,9,7,6],[11,9,0,4],[14,2,9,5],[0,5,7,3],[11,1,10,0],[13,15,6,9],[2,6,7,5],[10,0,2,14],[7,11,4,2],[0,10,3,7],[13,15,7,3],[8,11,7,4],[13,11,6,10],[13,2,0,7],[11,8,3,10],[5,1,14,8],[3,12,2,13],[4,1,10,2],[12,11,0,5],[2,13,3,4],[3,4,8,0],[15,13,7,0],[8,3,1,7],[7,8,3,14],[2,10,9,12],[13,0,8,10],[1,15,12,2],[10,12,0,1],[6,14,12,2],[1,6,12,13],[11,12,9,4],[13,9,8,12],[11,9,15,14],[11,0,13,1],[0,4,14,12],[3,4,10,5],[4,8,12,10]],[[13,6,5,10],[15,6,12,10],[8,14,0,10],[7,10,15,1],[2,8,11,9],[14,13,6,1],[8,12,6,10],[9,14,0,7],[2,10,12,0],[3,15,7,14],[9,1,0,10],[1,2,6,13],[5,2,7,14],[2,15,0,7],[8,5,9,13],[11,6,14,10],[14,8,4,12],[7,0,4,10],[1,11,5,0],[15,9,12,3],[12,14,7,4],[8,12,6,9],[11,6,3,15],[6,0,9,14],[15,8,12,3],[2,0,15,9],[11,0,5,3],[5,10,14,4],[13,9,5,1],[4,3,7,10],[8,9,7,2],[12,5,14,13],[8,9,14,0],[3,1,13,5],[4,10,8,15],[12,2,5,15],[10,1,5,7],[5,6,3,13],[6,8,0,9],[14,1,15,13],[4,13,15,2],[5,9,7,1],[8,4,6,9],[4,12,1,3],[12,10,15,4],[11,5,6,4],[11,4,5,7],[5,13,14,10],[12,5,15,10],[14,3,1,13],[8,9,15,13],[11,6,7,4],[2,7,9,8],[6,14,4,13],[9,5,10,11],[2,8,6,12],[8,11,9,15],[0,15,8,13],[14,10,3,7],[3,15,4,8],[2,9,13,5],[13,12,10,9],[0,8,12,7],[8,7,5,3],[3,13,14,1],[15,2,7,9],[8,6,9,7],[2,6,7,0],[8,13,11,15],[13,3,0,2],[4,2,11,15],[8,11,5,13],[13,12,11,6],[11,3,12,7],[6,1,13,5],[12,1,8,3],[4,3,5,0],[11,7,9,0],[1,2,10,7],[12,7,4,14],[7,0,15,11],[14,9,1,6],[8,7,10,15],[4,1,8,3],[15,2,12,7],[15,13,8,3],[6,15,12,9],[13,6,1,14],[2,4,5,1],[10,14,0,11],[8,9,13,12],[6,11,2,9],[14,3,13,2],[13,11,15,14],[2,0,4,11],[2,6,11,7],[8,9,2,11],[4,0,5,15],[4,7,13,6],[4,14,11,2],[5,11,14,8],[10,3,5,12],[1,15,14,4],[4,0,3,6],[0,12,9,10],[4,9,14,11],[6,14,10,5],[13,6,12,1],[7,13,0,9],[11,13,8,0],[5,13,4,7],[0,6,12,7],[9,10,7,5],[0,10,1,4],[2,12,1,14],[15,14,13,1],[7,1,11,2],[4,10,2,8],[2,3,12,4],[3,14,2,10],[8,12,0,11],[6,11,13,4],[12,5,4,1],[0,14,5,4],[14,3,2,4],[9,1,11,3],[9,3,10,12],[7,3,5,8]],[[9,13,10,7],[12,7,8,3],[4,15,12,13],[7,2,12,9],[2,11,15,3],[10,15,7,4],[0,5,11,7],[1,4,10,12],[15,8,4,6],[11,10,6,0],[15,8,10,13],[7,6,13,11],[14,12,13,2],[3,13,11,10],[0,6,1,11],[8,0,7,3],[3,14,13,15],[9,14,3,13],[13,4,10,5],[4,10,8,1],[13,15,0,4],[6,9,12,2],[1,3,10,15],[15,6,14,9],[0,12,14,5],[3,7,2,6],[11,0,4,8],[14,3,10,7],[9,13,4,7],[3,13,9,4],[2,1,10,6],[3,12,6,1],[4,15,3,7],[5,13,14,3],[13,8,1,7],[3,14,15,12],[12,1,5,9],[7,13,9,4],[8,0,6,7],[12,6,0,7],[6,13,4,12],[2,6,9,7],[14,10,8,6],[7,13,8,14],[3,5,8,10],[6,10,7,13],[15,13,4,11],[15,7,10,6],[15,3,5,14],[15,12,8,9],[12,5,0,6],[6,7,5,8],[1,11,15,0],[11,15,10,5],[3,4,1,5],[4,5,3,12],[5,14,6,8],[8,9,6,10],[11,1,4,5],[1,12,8,3],[10,0,3,4],[7,15,9,1],[10,11,8,0],[0,7,13,9],[15,3,4,13],[3,6,2,0],[8,4,13,12],[13,4,12,14],[1,4,6,8],[14,15,4,9],[7,12,10,15],[5,10,15,0],[5,9,12,3],[5,3,9,15],[1,4,9,6],[3,9,10,7],[12,10,11,5],[7,2,3,5],[6,10,9,0],[15,12,2,5],[6,4,10,3],[12,10,0,6],[6,15,2,3],[13,7,3,6],[5,11,4,0],[13,2,5,3],[13,1,6,12],[5,3,1,12],[6,0,10,15],[6,2,4,9],[0,14,8,15],[5,7,9,15],[11,4,14,15],[9,4,14,8],[0,4,2,5],[1,3,8,14],[0,3,15,11],[12,14,9,11],[14,4,1,10],[0,4,9,7],[9,10,12,3],[11,13,7,2],[8,14,13,4],[9,11,13,5],[1,14,11,12],[10,14,12,6],[9,7,8,14],[11,7,1,14],[2,11,15,14],[9,4,15,5],[3,5,15,8],[1,0,5,6],[12,5,15,2],[10,6,8,3],[0,10,9,4],[8,5,14,3],[3,1,14,15],[9,3,4,7],[14,13,0,5],[10,14,4,0],[12,4,3,0],[4,1,8,3],[8,6,14,3],[12,8,5,11],[9,2,10,8],[15,4,0,9],[12,10,14,6],[12,11,5,8]]]
ZW = 550
def setup_inputs(rng):
    return {"z": rng.standard_normal((N, 128, ZW), dtype=np.float32)}
def reference(z):
    y = np.zeros((N, 128, T), np.float64)
    fill = [0] * N
    for r in range(N):
        for t in range(T):
            for e in ROUTE[r][t]:
                y[r][:, t] += z[e][:, fill[e]].astype(np.float64)
                fill[e] += 1
    return {"y": y.astype(z.dtype)}

@@ -1,0 +1,130 @@
+from concourse.bass import DstId, RemoteDMATransfer
+
+NRANGE = 4
+ZW_MAX = 550
+
+SCRATCH = {
+    "zs": ("sbuf", [128, ZW_MAX], "float32"),
+    "rz": ("sbuf", [128, ZW_MAX], "float32"),
+    "land": ("sbuf", [128, 128], "float32"),
+    "out": ("sbuf", [128, 128], "float32"),
+}
+SEMAPHORES = ["loaded", "relayed", "arrived", "folded", "stored", "sent"]
+
+FOLDERS = {2: (3, 0, 4, 6), 3: (2, 1, 5, 7)}
+SENDER_SHIFT = {0: 0, 3: 0, 5: 0, 6: -2, 2: 2, 4: 2, 1: 4, 7: 4}
+
+
+def make_plan(cores, route):
+    n = len(cores)
+    nt = len(route[0])
+    per = nt // NRANGE
+    fill = [0] * n
+    col = {}
+    for r in range(n):
+        for t in range(nt):
+            for e in route[r][t]:
+                col[(e, r, t)] = fill[e]
+                fill[e] += 1
+    relays = {}
+    n_relay = {}
+    sends = {}
+    n_arr = {}
+    folds = {}
+    need = {}
+    for r in range(n):
+        owner = cores[r]
+        base = owner - owner % 8
+        for j in range(NRANGE):
+            folder = base + FOLDERS[owner % 8][j]
+            where = {}
+            nxt = 0
+            for e in range(n):
+                cs = [col[(e, r, t)] for t in range(j * per, (j + 1) * per) if e in route[r][t]]
+                if not cs:
+                    continue
+                lo, hi = cs[0], cs[-1] + 1
+                ecore = cores[e]
+                if ecore == folder:
+                    where[e] = ("zs", lo)
+                    continue
+                d = (owner // 8 - ecore // 8) % 8
+                sender = ecore + SENDER_SHIFT[d]
+                src = "zs" if sender == ecore else "rz"
+                sends.setdefault(sender, []).append((folder, src, lo, hi, nxt))
+                if sender != ecore:
+                    need.setdefault((ecore, sender), []).append((lo, hi))
+                n_arr[folder] = n_arr.get(folder, 0) + (16 if sender // 8 == folder // 8 else 8)
+                where[e] = ("land", nxt - lo)
+                nxt += hi - lo
+            toks = []
+            for t in range(j * per, (j + 1) * per):
+                srcs = []
+                for e in route[r][t]:
+                    buf, shift = where[e]
+                    srcs.append((buf, col[(e, r, t)] + (shift if buf == "land" else 0)))
+                toks.append((t, srcs))
+            folds[folder] = (owner, toks)
+    for (ecore, sender), blocks in sorted(need.items()):
+        blocks = sorted(blocks)
+        merged = [list(blocks[0])]
+        for lo, hi in blocks[1:]:
+            if lo == merged[-1][1]:
+                merged[-1][1] = hi
+            else:
+                merged.append([lo, hi])
+        for lo, hi in merged:
+            relays.setdefault(ecore, []).append((sender, lo, hi))
+            n_relay[sender] = n_relay.get(sender, 0) + 1
+    return {"relays": relays, "n_relay": n_relay, "sends": sends, "n_arr": n_arr, "folds": folds, "used": fill}
+
+
+PLAN_CACHE = {}
+
+
+def rank_program(g, core, T, topo):
+    if "p" not in PLAN_CACHE:
+        PLAN_CACHE["p"] = make_plan(list(T.cores), T.tables["ROUTE"])
+    plan = PLAN_CACHE["p"]
+    rank = T.rank_of(core)
+    sem = T.sem
+    sent = 0
+
+    if rank is not None:
+        used = plan["used"][rank]
+        g.sync.dma_start(T.zs[:, 0:used], T.z[:, 0:used]).then_inc(sem.loaded, 16)
+        g.wait_ge(sem.loaded, 16)
+        for dst, lo, hi in plan["relays"].get(core, []):
+            rid, pid, _se = topo.addr(dst)
+            g.remote_dma(T.rz[:, lo:hi], T.zs[:, lo:hi], sem.relayed, sem.sent, pid, rid, topo.mask(core, dst))
+            sent += 16
+    elif core in plan["n_relay"]:
+        g.wait_ge(sem.relayed, 16 * plan["n_relay"][core])
+
+    todo = sorted(plan["sends"].get(core, []), key=lambda s: s[0] // 8 == core // 8)
+    for dst, src, lo, hi, at in todo:
+        rid, pid, _se = topo.addr(dst)
+        m = topo.mask(core, dst)
+        g.remote_dma(T.land[:, at:at + hi - lo], T[src][:, lo:hi], sem.arrived, sem.sent, pid, rid, m)
+        sent += 16 if m == 0xFFFF else 8
+
+    if core in plan["folds"]:
+        owner, toks = plan["folds"][core]
+        rid, pid, _se = topo.addr(owner)
+        g.wait_ge(sem.arrived, plan["n_arr"][core])
+        for k in range(0, len(toks), 16):
+            trs = []
+            for i, (t, srcs) in enumerate(toks[k:k + 16]):
+                trs.append(RemoteDMATransfer(
+                    dst_ids=[DstId(rid=rid, pnc=pid)], dma_engine_mask=1 << i, remote_sem=sem.folded,
+                    srcs=[T[buf][:, c:c + 1] for buf, c in srcs], dsts=[T.out[:, t:t + 1]], alu_op=1))
+                sent += 1
+            g.remote_dma_fused(trs, local_sem=sem.sent)
+
+    if rank is not None:
+        g.sync.wait_ge(sem.folded, len(T.tables["ROUTE"][rank]))
+        g.sync.dma_start(T.y[:, :], T.out[:, :]).then_inc(sem.stored, 16)
+        g.sync.wait_ge(sem.stored, 16)
+
+    if sent:
+        g.wait_ge(sem.sent, sent)

@@ -2,6 +2,9 @@ from concourse.bass import DstId, RemoteDMATransfer
 
 NRANGE = 4
 ZW_MAX = 550
+OFF_CHIP = 0x00FF
+UPPER = 0xFF00
+SEND_ENGINES = 8
 
 SCRATCH = {
     "zs": ("sbuf", [128, ZW_MAX], "float32"),
@@ -46,7 +49,7 @@ def make_plan(cores, route):
                 lo, hi = cs[0], cs[-1] + 1
                 ecore = cores[e]
                 if ecore == folder:
-                    where[e] = ("zs", lo)
+                    where[e] = ("zs", 0)
                     continue
                 d = (owner // 8 - ecore // 8) % 8
                 sender = ecore + SENDER_SHIFT[d]
@@ -54,18 +57,14 @@ def make_plan(cores, route):
                 sends.setdefault(sender, []).append((folder, src, lo, hi, nxt))
                 if sender != ecore:
                     need.setdefault((ecore, sender), []).append((lo, hi))
-                n_arr[folder] = n_arr.get(folder, 0) + (16 if sender // 8 == folder // 8 else 8)
+                n_arr[folder] = n_arr.get(folder, 0) + 1
                 where[e] = ("land", nxt - lo)
                 nxt += hi - lo
             toks = []
             for t in range(j * per, (j + 1) * per):
-                srcs = []
-                for e in route[r][t]:
-                    buf, shift = where[e]
-                    srcs.append((buf, col[(e, r, t)] + (shift if buf == "land" else 0)))
-                toks.append((t, srcs))
+                toks.append((t, [(where[e][0], col[(e, r, t)] + where[e][1]) for e in route[r][t]]))
             folds[folder] = (owner, toks)
-    for (ecore, sender), blocks in sorted(need.items()):
+    for (ecore, sender), blocks in sorted(need.items(), key=lambda kv: (kv[0][0], -kv[0][1])):
         blocks = sorted(blocks)
         merged = [list(blocks[0])]
         for lo, hi in blocks[1:]:
@@ -104,14 +103,14 @@ def rank_program(g, core, T, topo):
     todo = sorted(plan["sends"].get(core, []), key=lambda s: s[0] // 8 == core // 8)
     for dst, src, lo, hi, at in todo:
         rid, pid, _se = topo.addr(dst)
-        m = topo.mask(core, dst)
+        m = UPPER if topo.chip(dst) == topo.chip(core) else OFF_CHIP
         g.remote_dma(T.land[:, at:at + hi - lo], T[src][:, lo:hi], sem.arrived, sem.sent, pid, rid, m)
-        sent += 16 if m == 0xFFFF else 8
+        sent += SEND_ENGINES
 
     if core in plan["folds"]:
         owner, toks = plan["folds"][core]
         rid, pid, _se = topo.addr(owner)
-        g.wait_ge(sem.arrived, plan["n_arr"][core])
+        g.wait_ge(sem.arrived, SEND_ENGINES * plan["n_arr"][core])
         for k in range(0, len(toks), 16):
             trs = []
             for i, (t, srcs) in enumerate(toks[k:k + 16]):

from concourse.bass import DstId, RemoteDMATransfer

NRANGE = 4
ZW_MAX = 550
OFF_CHIP = 0x00FF
UPPER = 0xFF00
SEND_ENGINES = 8

SCRATCH = {
    "zs": ("sbuf", [128, ZW_MAX], "float32"),
    "rz": ("sbuf", [128, ZW_MAX], "float32"),
    "land": ("sbuf", [128, 128], "float32"),
    "out": ("sbuf", [128, 128], "float32"),
}
SEMAPHORES = ["loaded", "relayed", "arrived", "folded", "stored", "sent"]

FOLDERS = {2: (3, 0, 4, 6), 3: (2, 1, 5, 7)}
SENDER_SHIFT = {0: 0, 3: 0, 5: 0, 6: -2, 2: 2, 4: 2, 1: 4, 7: 4}


def make_plan(cores, route):
    n = len(cores)
    nt = len(route[0])
    per = nt // NRANGE
    fill = [0] * n
    col = {}
    for r in range(n):
        for t in range(nt):
            for e in route[r][t]:
                col[(e, r, t)] = fill[e]
                fill[e] += 1
    relays = {}
    n_relay = {}
    sends = {}
    n_arr = {}
    folds = {}
    need = {}
    for r in range(n):
        owner = cores[r]
        base = owner - owner % 8
        for j in range(NRANGE):
            folder = base + FOLDERS[owner % 8][j]
            where = {}
            nxt = 0
            for e in range(n):
                cs = [col[(e, r, t)] for t in range(j * per, (j + 1) * per) if e in route[r][t]]
                if not cs:
                    continue
                lo, hi = cs[0], cs[-1] + 1
                ecore = cores[e]
                if ecore == folder:
                    where[e] = ("zs", 0)
                    continue
                d = (owner // 8 - ecore // 8) % 8
                sender = ecore + SENDER_SHIFT[d]
                src = "zs" if sender == ecore else "rz"
                sends.setdefault(sender, []).append((folder, src, lo, hi, nxt))
                if sender != ecore:
                    need.setdefault((ecore, sender), []).append((lo, hi))
                n_arr[folder] = n_arr.get(folder, 0) + 1
                where[e] = ("land", nxt - lo)
                nxt += hi - lo
            toks = []
            for t in range(j * per, (j + 1) * per):
                toks.append((t, [(where[e][0], col[(e, r, t)] + where[e][1]) for e in route[r][t]]))
            folds[folder] = (owner, toks)
    for (ecore, sender), blocks in sorted(need.items(), key=lambda kv: (kv[0][0], -kv[0][1])):
        blocks = sorted(blocks)
        merged = [list(blocks[0])]
        for lo, hi in blocks[1:]:
            if lo == merged[-1][1]:
                merged[-1][1] = hi
            else:
                merged.append([lo, hi])
        for lo, hi in merged:
            relays.setdefault(ecore, []).append((sender, lo, hi))
            n_relay[sender] = n_relay.get(sender, 0) + 1
    return {"relays": relays, "n_relay": n_relay, "sends": sends, "n_arr": n_arr, "folds": folds, "used": fill}


PLAN_CACHE = {}


def rank_program(g, core, T, topo):
    if "p" not in PLAN_CACHE:
        PLAN_CACHE["p"] = make_plan(list(T.cores), T.tables["ROUTE"])
    plan = PLAN_CACHE["p"]
    rank = T.rank_of(core)
    sem = T.sem
    sent = 0

    if rank is not None:
        used = plan["used"][rank]
        g.sync.dma_start(T.zs[:, 0:used], T.z[:, 0:used]).then_inc(sem.loaded, 16)
        g.wait_ge(sem.loaded, 16)
        for dst, lo, hi in plan["relays"].get(core, []):
            rid, pid, _se = topo.addr(dst)
            g.remote_dma(T.rz[:, lo:hi], T.zs[:, lo:hi], sem.relayed, sem.sent, pid, rid, topo.mask(core, dst))
            sent += 16
    elif core in plan["n_relay"]:
        g.wait_ge(sem.relayed, 16 * plan["n_relay"][core])

    todo = sorted(plan["sends"].get(core, []), key=lambda s: s[0] // 8 == core // 8)
    for dst, src, lo, hi, at in todo:
        rid, pid, _se = topo.addr(dst)
        m = UPPER if topo.chip(dst) == topo.chip(core) else OFF_CHIP
        g.remote_dma(T.land[:, at:at + hi - lo], T[src][:, lo:hi], sem.arrived, sem.sent, pid, rid, m)
        sent += SEND_ENGINES

    if core in plan["folds"]:
        owner, toks = plan["folds"][core]
        rid, pid, _se = topo.addr(owner)
        g.wait_ge(sem.arrived, SEND_ENGINES * plan["n_arr"][core])
        for k in range(0, len(toks), 16):
            trs = []
            for i, (t, srcs) in enumerate(toks[k:k + 16]):
                trs.append(RemoteDMATransfer(
                    dst_ids=[DstId(rid=rid, pnc=pid)], dma_engine_mask=1 << i, remote_sem=sem.folded,
                    srcs=[T[buf][:, c:c + 1] for buf, c in srcs], dsts=[T.out[:, t:t + 1]], alu_op=1))
                sent += 1
            g.remote_dma_fused(trs, local_sem=sem.sent)

    if rank is not None:
        g.sync.wait_ge(sem.folded, len(T.tables["ROUTE"][rank]))
        g.sync.dma_start(T.y[:, :], T.out[:, :]).then_inc(sem.stored, 16)
        g.sync.wait_ge(sem.stored, 16)

    if sent:
        g.wait_ge(sem.sent, sent)
